import numpy as np
import ml_dtypes


def mxq(x, axis, fmt="e4m3"):
    dtype, down = {"e4m3": (ml_dtypes.float8_e4m3fn, 7), "e5m2": (ml_dtypes.float8_e5m2, 14)}[fmt]
    v = np.moveaxis(np.asarray(x, np.float32).astype(ml_dtypes.bfloat16).astype(np.float64), axis, -1)
    blocks = v.reshape(v.shape[:-1] + (-1, 32))
    amax = np.abs(blocks).max(-1, keepdims=True)
    byte = np.maximum(np.where(amax > 0, np.frexp(amax)[1] - 1 + 127, 0) - down, 1)
    scale = np.exp2(byte - 127.0)
    codes = (blocks / scale).astype(np.float32).astype(dtype).astype(np.float64)
    return np.moveaxis((codes * scale).reshape(v.shape), -1, axis)


WIDE = False


def mx_kscale(k):
    if not WIDE:
        return np.ones(k)
    levels = np.array([24, -24, 12, -12, 0])
    if k % 512:
        return np.exp2(np.random.permutation(np.resize(levels, k // 32))).repeat(32)
    a = np.empty((k // 512, 16))
    for p in range(k // 512):
        a[p, :8] = np.random.permutation(np.resize(levels, 8))
        for g in range(8):
            far = levels[np.abs(levels - a[p, g]) >= 10]
            a[p, g + 8] = far[np.random.randint(len(far))]
    return np.exp2(a.ravel()).repeat(32)


def f64(x):
    return np.asarray(x).astype(np.float64)


def striped8(idx):
    return np.concatenate([v.reshape(-1, 16).T for v in idx]).astype(np.uint16)


def unstriped8(offs):
    return np.stack([offs[16 * g:16 * g + 16].T.reshape(-1) for g in range(8)]).astype(np.int64)


def planes(y):
    n, m = y.shape
    v = y.astype(np.float32).astype(ml_dtypes.bfloat16).astype(np.float64).reshape(n // 32, 32, m)
    top = np.abs(v).max(1)
    byte = np.clip(np.where(top > 0, np.frexp(top)[1] - 1 + 127 - 7, 1), 1, 254)
    codes = (v * np.exp2(127.0 - byte)[:, None, :]).reshape(n, m).astype(np.float32).astype(ml_dtypes.float8_e4m3fn).view(np.uint8)
    words = codes.reshape(n // 512, 128, 4, m).transpose(0, 1, 3, 2)
    return np.ascontiguousarray(words), np.ascontiguousarray(byte.astype(np.uint8).reshape(n // 512, 16, m))


def silu(f):
    return f / (1.0 + np.exp(-np.maximum(f, -700.0)))


K, L, N, T, J = 512, 512, 512, 2048, 1024


def setup_inputs():
    n = np.random.standard_normal
    s = mx_kscale(K)[:, None]
    s2 = mx_kscale(L)[:, None]
    return {
        "xT": (n((K, T)) * s).astype(np.float32),
        "wgt": np.repeat(np.random.uniform(0.5, 2.0, (8, J)), 16, axis=0).astype(np.float32),
        "zT": (n((L, T)) * s2).astype(np.float32),
        "wgt2": np.repeat(np.random.uniform(0.5, 2.0, (8, J)), 16, axis=0).astype(np.float32),
        "wa": (n((K, N)) / np.sqrt(K) / s).astype(np.float32),
        "wb": (n((L, N)) / np.sqrt(L) / s2).astype(np.float32),
        "b": (0.3 * n(N)).astype(np.float32),
        "offs": striped8(np.stack([np.random.permutation(T)[:J] for _ in range(8)])),
        "offs2": striped8(np.stack([np.random.permutation(T)[:J] for _ in range(8)])),
    }


def reference(xT, wgt, zT, wgt2, wa, wb, b, offs, offs2):
    idx = unstriped8(offs)
    idx2 = unstriped8(offs2)
    rows = np.arange(K)
    xg = f64(wgt)[rows // 4 % 128] * f64(xT)[rows[:, None], idx[rows % 512 // 64]]
    xT_ = mxq(xg, 0, "e4m3")
    rows = np.arange(L)
    xg = f64(wgt2)[rows // 4 % 128] * f64(zT)[rows[:, None], idx2[rows % 512 // 64]]
    zT_ = mxq(xg, 0, "e4m3")
    wa_ = mxq(f64(wa), 0, "e4m3")
    wb_ = mxq(f64(wb), 0, "e4m3")
    ya = wa_.T @ xT_
    yb = wb_.T @ zT_
    out_0 = silu(ya * yb + f64(b)[:, None])
    return (out_0,) + planes(out_0)

@@ -1,0 +1,209 @@
+from contextlib import ExitStack
+
+import concourse.mybir as mybir
+from concourse.masks import make_identity
+
+K, L, N, T, J = 512, 512, 512, 2048, 1024
+FLOPS = 2 * (K + L) * N * J
+
+F32 = mybir.dt.float32
+BF16 = mybir.dt.bfloat16
+I32 = mybir.dt.int32
+U32 = mybir.dt.uint32
+U16 = mybir.dt.uint16
+U8 = mybir.dt.uint8
+FP8X4 = mybir.dt.float8_e4m3fn_x4
+MULT = mybir.AluOpType.mult
+SILU = mybir.ActivationFunctionType.Silu
+
+P = 128
+PACK = 4
+BANK = 512
+LIST_ROWS = 16
+RUN = 4
+X_CHUNK = 512
+Z_CHUNK = 256
+HEADS = 8
+SEGS = J // P
+
+
+def tile_list_mul_siluP_kernel(
+    tc, xT, wgt, zT, wgt2, wa, wb, b, offs, offs2, out_0, out_1, out_2
+):
+    nc = tc.nc
+    with ExitStack() as ctx:
+        lists = ctx.enter_context(tc.tile_pool(name="lists", bufs=1))
+        keep = ctx.enter_context(tc.tile_pool(name="keep", bufs=1))
+        psum = ctx.enter_context(tc.psum_pool(name="psum", bufs=8))
+
+        def load_rows(src, i, name):
+            rows = keep.tile([P, T], F32, name=name)
+            nc.sync.dma_start(out=rows[:], in_=src.rearrange("(p i) t -> p i t", i=PACK)[:, i, :])
+            return rows
+
+        def load_weight(src, name):
+            raw = keep.tile([P, PACK, N], F32, name=name)
+            nc.sync.dma_start(out=raw[:], in_=src.rearrange("(p i) n -> p i n", i=PACK))
+            return raw
+
+        def gather(picked, i, rows, offsets, gain, j0, width):
+            cols = slice(j0, j0 + width)
+            nc.vector.tensor_tensor(
+                picked[:, i, cols],
+                rows[:].indirect(offsets[:, j0 // LIST_ROWS : (j0 + width) // LIST_ROWS]),
+                gain[:, cols],
+                MULT,
+            )
+
+        def copy_on(engine, out, in_):
+            if engine == "scalar":
+                nc.scalar.copy(out, in_)
+            else:
+                nc.vector.tensor_copy(out, in_)
+
+        def weave(engine, src, name):
+            width = src.shape[2]
+            woven = keep.tile([P, width * PACK], BF16, name=name, align_bytes=64)
+            copy_on(
+                engine,
+                woven[:].rearrange("p (c r i) -> p c i r", r=RUN, i=PACK),
+                src.rearrange("p i (c r) -> p c i r", r=RUN),
+            )
+            return woven
+
+        def weave_weight(engine, raw, name):
+            woven = keep.tile([P, N * PACK], BF16, name=name, align_bytes=64)
+            copy_on(
+                engine,
+                woven[:].rearrange("p (t m i) -> p m i t", t=PACK, i=PACK),
+                raw[:].rearrange("p i (m t) -> p m i t", t=PACK),
+            )
+            return woven
+
+        def quantize(woven, name):
+            width = woven.shape[1] // PACK
+            codes = keep.tile([P, width], U32, name=name + "_codes", align_bytes=64)
+            scales = keep.tile([P, width], U8, name=name + "_scales", align_bytes=64)
+            nc.vector.quantize_mx(out=codes[:].bitcast(FP8X4), scales=scales[:], in_=woven[:])
+            return codes, scales
+
+        def project(acc, weight, t, moving):
+            cols = slice(t * P, (t + 1) * P)
+            nc.tensor.matmul_mx(
+                out=acc,
+                lhsT=weight[0][:, cols].bitcast(FP8X4),
+                lhsT_scale=weight[1][:, cols],
+                rhs=moving[0][:].bitcast(FP8X4),
+                rhs_scale=moving[1][:],
+                start=True,
+                stop=True,
+            )
+
+        x_list = lists.tile([P, J // LIST_ROWS], U16, name="x_list")
+        z_list = lists.tile([P, J // LIST_ROWS], U16, name="z_list")
+        bias = keep.tile([P, PACK], F32, name="bias")
+        x_gain = keep.tile([P, J], F32, name="x_gain")
+        z_gain = keep.tile([P, J], F32, name="z_gain")
+        per_turn = BANK // P
+        live = HEADS * SEGS
+        folded = keep.tile([P, P], F32, name="folded")
+        nc.gpsimd.memset(folded[live:P, :], 0.0)
+        nc.sync.dma_start(x_list[:], offs)
+        nc.sync.dma_start(out=x_gain[:, 0:BANK], in_=wgt[:, 0:BANK])
+        x_rows = [load_rows(xT, 0, "x_rows0")]
+        nc.sync.dma_start(out=x_gain[:, BANK:J], in_=wgt[:, BANK:J])
+        nc.sync.dma_start(
+            out=folded[0:live, :], in_=wgt2.rearrange("(g s) (r c) -> s g r c", s=LIST_ROWS, c=P)[0]
+        )
+        for i in range(1, PACK):
+            x_rows.append(load_rows(xT, i, "x_rows%d" % i))
+        nc.sync.dma_start(z_list[:], offs2)
+        nc.sync.dma_start(out=bias[:], in_=b.rearrange("(p t) -> p t", t=PACK))
+        z_rows = [load_rows(zT, 0, "z_rows0")]
+        wa_raw = load_weight(wa, "wa_raw")
+        for i in range(1, PACK):
+            z_rows.append(load_rows(zT, i, "z_rows%d" % i))
+        wb_raw = load_weight(wb, "wb_raw")
+
+        ident = keep.tile([P, P], F32, name="ident")
+        make_identity(nc, ident[:])
+        warm = keep.tile([P, 1], F32, name="warm")
+        nc.scalar.activation(warm[:], ident[:, 0:1], SILU)
+
+        turned = psum.tile([P, BANK], F32, name="acc")
+        nc.tensor.transpose(turned[:, 0:P], folded[:], ident[:])
+        by_seg = turned[:, 0:live].rearrange("c (g r) -> c r g", r=SEGS)
+        spread = keep.tile([P, SEGS, P], F32, name="spread")
+        nc.scalar.copy(
+            spread[:].rearrange("c r (g s) -> c r g s", s=LIST_ROWS),
+            by_seg.unsqueeze(3).to_broadcast([P, SEGS, HEADS, LIST_ROWS]),
+        )
+        for h in range(SEGS // per_turn):
+            back = psum.tile([P, BANK], F32, name="acc")
+            for r in range(per_turn):
+                nc.tensor.transpose(back[:, r * P : (r + 1) * P], spread[:, h * per_turn + r, :], ident[:])
+            nc.scalar.copy(z_gain[:, h * BANK : (h + 1) * BANK], back[:])
+
+        x_picked = keep.tile([P, PACK, J], F32, name="x_picked")
+        gather(x_picked, 0, x_rows[0], x_list, x_gain, 0, J // 2)
+        gather(x_picked, 0, x_rows[0], x_list, x_gain, J // 2, J // 2)
+        gather(x_picked, 1, x_rows[1], x_list, x_gain, 0, J)
+        gather(x_picked, 2, x_rows[2], x_list, x_gain, 0, J)
+        x_woven = []
+        for c in range(J // X_CHUNK):
+            gather(x_picked, 3, x_rows[3], x_list, x_gain, c * X_CHUNK, X_CHUNK)
+            x_woven.append(weave("scalar", x_picked[:, :, c * X_CHUNK : (c + 1) * X_CHUNK], "x_woven%d" % c))
+        z_picked = keep.tile([P, PACK, J], F32, name="z_picked")
+        gather(z_picked, 0, z_rows[0], z_list, z_gain, 0, J)
+        wa_mx = quantize(weave_weight("vector", wa_raw, "wa_woven"), "wa")
+        ya = keep.tile([P, PACK, J], F32, name="ya")
+        for c in range(J // X_CHUNK):
+            x_mx = quantize(x_woven[c], "x%d" % c)
+            for t in range(PACK):
+                acc = psum.tile([P, BANK], F32, name="acc")
+                project(acc[:], wa_mx, t, x_mx)
+                nc.scalar.copy(ya[:, t, c * X_CHUNK : (c + 1) * X_CHUNK], acc[:])
+
+        for i in range(1, PACK - 1):
+            gather(z_picked, i, z_rows[i], z_list, z_gain, 0, J)
+        chunks = J // Z_CHUNK
+        z_woven = []
+        for c in range(chunks):
+            gather(z_picked, 3, z_rows[3], z_list, z_gain, c * Z_CHUNK, Z_CHUNK)
+            z_woven.append(weave("scalar", z_picked[:, :, c * Z_CHUNK : (c + 1) * Z_CHUNK], "z_woven%d" % c))
+        wb_mx = quantize(weave_weight("vector", wb_raw, "wb_woven"), "wb")
+
+        y_codes = keep.tile([P, J], U32, name="y_codes", align_bytes=64)
+        y_scales = keep.tile([P, J], U8, name="y_scales", align_bytes=64)
+        out_rows = out_0.rearrange("(p t) j -> p t j", t=PACK)
+        out_words = out_1.rearrange("a p j i -> p (a j i)").bitcast(I32)
+        out_scales = out_2.rearrange("a q j -> q (a j)").bitcast(I32)
+        per_bank = BANK // Z_CHUNK
+        z_mx = [quantize(z_woven[c], "z%d" % c) for c in range(chunks)]
+        ys = []
+        for c in range(chunks):
+            cols = slice(c * Z_CHUNK, (c + 1) * Z_CHUNK)
+            prod = keep.tile([P, PACK, Z_CHUNK], F32, name="prod%d" % c)
+            y = keep.tile([P, PACK, Z_CHUNK], F32, name="y%d" % c)
+            for t0 in range(0, PACK, per_bank):
+                acc = psum.tile([P, BANK], F32, name="acc")
+                for u in range(per_bank):
+                    project(acc[:, u * Z_CHUNK : (u + 1) * Z_CHUNK], wb_mx, t0 + u, z_mx[c])
+                nc.vector.tensor_tensor(
+                    prod[:, t0 : t0 + per_bank, :],
+                    acc[:].rearrange("p (u j) -> p u j", u=per_bank),
+                    ya[:, t0 : t0 + per_bank, cols],
+                    MULT,
+                )
+                for t in range(t0, t0 + per_bank):
+                    nc.scalar.activation(y[:, t, :], prod[:, t, :], SILU, bias=bias[:, t : t + 1])
+            nc.sync.dma_start(out=out_rows[:, :, cols], in_=y[:])
+            ys.append(y)
+        for c in range(chunks):
+            cols = slice(c * Z_CHUNK, (c + 1) * Z_CHUNK)
+            y_woven = weave("scalar" if c == 0 else "vector", ys[c][:], "y_woven%d" % c)
+            nc.vector.quantize_mx(out=y_codes[:, cols].bitcast(FP8X4), scales=y_scales[:, cols], in_=y_woven[:])
+            nc.sync.dma_start(out=out_words[:, cols], in_=y_codes[:, cols].bitcast(I32))
+        for q in range(4):
+            queue = nc.sync if q % 2 == 0 else nc.scalar
+            queue.dma_start(out=out_scales[4 * q : 4 * q + 4, :], in_=y_scales[32 * q : 32 * q + 4, :].bitcast(I32))

@@ -22,7 +22,7 @@ BANK = 512
 LIST_ROWS = 16
 RUN = 4
 X_CHUNK = 512
-Z_CHUNK = 256
+Z_WIDTHS = (256, 256, 256, 256)
 HEADS = 8
 SEGS = J // P
 
@@ -37,12 +37,12 @@ def tile_list_mul_siluP_kernel(
         psum = ctx.enter_context(tc.psum_pool(name="psum", bufs=8))
 
         def load_rows(src, i, name):
-            rows = keep.tile([P, T], F32, name=name)
+            rows = keep.tile([P, T], F32, name=name, tag=name, align_bytes=64)
             nc.sync.dma_start(out=rows[:], in_=src.rearrange("(p i) t -> p i t", i=PACK)[:, i, :])
             return rows
 
         def load_weight(src, name):
-            raw = keep.tile([P, PACK, N], F32, name=name)
+            raw = keep.tile([P, PACK, N], F32, name=name, tag=name, align_bytes=64)
             nc.sync.dma_start(out=raw[:], in_=src.rearrange("(p i) n -> p i n", i=PACK))
             return raw
 
@@ -80,9 +80,9 @@ def tile_list_mul_siluP_kernel(
             )
             return woven
 
-        def quantize(woven, name):
+        def quantize(woven, name, slot=None):
             width = woven.shape[1] // PACK
-            codes = keep.tile([P, width], U32, name=name + "_codes", align_bytes=64)
+            codes = keep.tile([P, width], U32, name=name + "_codes", tag=slot or name + "_codes", align_bytes=64)
             scales = keep.tile([P, width], U8, name=name + "_scales", align_bytes=64)
             nc.vector.quantize_mx(out=codes[:].bitcast(FP8X4), scales=scales[:], in_=woven[:])
             return codes, scales
@@ -119,11 +119,11 @@ def tile_list_mul_siluP_kernel(
             x_rows.append(load_rows(xT, i, "x_rows%d" % i))
         nc.sync.dma_start(z_list[:], offs2)
         nc.sync.dma_start(out=bias[:], in_=b.rearrange("(p t) -> p t", t=PACK))
-        z_rows = [load_rows(zT, 0, "z_rows0")]
         wa_raw = load_weight(wa, "wa_raw")
-        for i in range(1, PACK):
-            z_rows.append(load_rows(zT, i, "z_rows%d" % i))
+        z_rows = [load_rows(zT, i, "z_rows%d" % i) for i in range(2)]
         wb_raw = load_weight(wb, "wb_raw")
+        for i in range(2, PACK):
+            z_rows.append(load_rows(zT, i, "z_rows%d" % i))
 
         ident = keep.tile([P, P], F32, name="ident")
         make_identity(nc, ident[:])
@@ -153,12 +153,12 @@ def tile_list_mul_siluP_kernel(
         for c in range(J // X_CHUNK):
             gather(x_picked, 3, x_rows[3], x_list, x_gain, c * X_CHUNK, X_CHUNK)
             x_woven.append(weave("scalar", x_picked[:, :, c * X_CHUNK : (c + 1) * X_CHUNK], "x_woven%d" % c))
+        wa_mx = quantize(weave_weight("vector", wa_raw, "wa_woven"), "wa")
         z_picked = keep.tile([P, PACK, J], F32, name="z_picked")
         gather(z_picked, 0, z_rows[0], z_list, z_gain, 0, J)
-        wa_mx = quantize(weave_weight("vector", wa_raw, "wa_woven"), "wa")
         ya = keep.tile([P, PACK, J], F32, name="ya")
         for c in range(J // X_CHUNK):
-            x_mx = quantize(x_woven[c], "x%d" % c)
+            x_mx = quantize(x_woven[c], "x%d" % c, ("wa_raw", "z_rows0")[c])
             for t in range(PACK):
                 acc = psum.tile([P, BANK], F32, name="acc")
                 project(acc[:], wa_mx, t, x_mx)
@@ -166,29 +166,30 @@ def tile_list_mul_siluP_kernel(
 
         for i in range(1, PACK - 1):
             gather(z_picked, i, z_rows[i], z_list, z_gain, 0, J)
-        chunks = J // Z_CHUNK
+        wb_woven = weave_weight("scalar", wb_raw, "wb_woven")
+        spans = [slice(sum(Z_WIDTHS[:c]), sum(Z_WIDTHS[: c + 1])) for c in range(len(Z_WIDTHS))]
         z_woven = []
-        for c in range(chunks):
-            gather(z_picked, 3, z_rows[3], z_list, z_gain, c * Z_CHUNK, Z_CHUNK)
-            z_woven.append(weave("scalar", z_picked[:, :, c * Z_CHUNK : (c + 1) * Z_CHUNK], "z_woven%d" % c))
-        wb_mx = quantize(weave_weight("vector", wb_raw, "wb_woven"), "wb")
+        for c, cols in enumerate(spans):
+            gather(z_picked, 3, z_rows[3], z_list, z_gain, cols.start, Z_WIDTHS[c])
+            z_woven.append(weave("scalar", z_picked[:, :, cols], "z_woven%d" % c))
+        wb_mx = quantize(wb_woven, "wb", "z_rows3")
 
         y_codes = keep.tile([P, J], U32, name="y_codes", align_bytes=64)
         y_scales = keep.tile([P, J], U8, name="y_scales", align_bytes=64)
         out_rows = out_0.rearrange("(p t) j -> p t j", t=PACK)
         out_words = out_1.rearrange("a p j i -> p (a j i)").bitcast(I32)
         out_scales = out_2.rearrange("a q j -> q (a j)").bitcast(I32)
-        per_bank = BANK // Z_CHUNK
-        z_mx = [quantize(z_woven[c], "z%d" % c) for c in range(chunks)]
+        z_mx = [quantize(z_woven[c], "z%d" % c) for c in range(len(spans))]
         ys = []
-        for c in range(chunks):
-            cols = slice(c * Z_CHUNK, (c + 1) * Z_CHUNK)
-            prod = keep.tile([P, PACK, Z_CHUNK], F32, name="prod%d" % c)
-            y = keep.tile([P, PACK, Z_CHUNK], F32, name="y%d" % c)
+        for c, cols in enumerate(spans):
+            width = Z_WIDTHS[c]
+            per_bank = BANK // width
+            prod = keep.tile([P, PACK, width], F32, name="prod%d" % c)
+            y = keep.tile([P, PACK, width], F32, name="y%d" % c)
             for t0 in range(0, PACK, per_bank):
                 acc = psum.tile([P, BANK], F32, name="acc")
                 for u in range(per_bank):
-                    project(acc[:, u * Z_CHUNK : (u + 1) * Z_CHUNK], wb_mx, t0 + u, z_mx[c])
+                    project(acc[:, u * width : (u + 1) * width], wb_mx, t0 + u, z_mx[c])
                 nc.vector.tensor_tensor(
                     prod[:, t0 : t0 + per_bank, :],
                     acc[:].rearrange("p (u j) -> p u j", u=per_bank),
@@ -199,8 +200,7 @@ def tile_list_mul_siluP_kernel(
                     nc.scalar.activation(y[:, t, :], prod[:, t, :], SILU, bias=bias[:, t : t + 1])
             nc.sync.dma_start(out=out_rows[:, :, cols], in_=y[:])
             ys.append(y)
-        for c in range(chunks):
-            cols = slice(c * Z_CHUNK, (c + 1) * Z_CHUNK)
+        for c, cols in enumerate(spans):
             y_woven = weave("scalar" if c == 0 else "vector", ys[c][:], "y_woven%d" % c)
             nc.vector.quantize_mx(out=y_codes[:, cols].bitcast(FP8X4), scales=y_scales[:, cols], in_=y_woven[:])
             nc.sync.dma_start(out=out_words[:, cols], in_=y_codes[:, cols].bitcast(I32))

from contextlib import ExitStack

import concourse.mybir as mybir
from concourse.masks import make_identity

K, L, N, T, J = 512, 512, 512, 2048, 1024
FLOPS = 2 * (K + L) * N * J

F32 = mybir.dt.float32
BF16 = mybir.dt.bfloat16
I32 = mybir.dt.int32
U32 = mybir.dt.uint32
U16 = mybir.dt.uint16
U8 = mybir.dt.uint8
FP8X4 = mybir.dt.float8_e4m3fn_x4
MULT = mybir.AluOpType.mult
SILU = mybir.ActivationFunctionType.Silu

P = 128
PACK = 4
BANK = 512
LIST_ROWS = 16
RUN = 4
X_CHUNK = 512
Z_WIDTHS = (256, 256, 256, 256)
HEADS = 8
SEGS = J // P


def tile_list_mul_siluP_kernel(
    tc, xT, wgt, zT, wgt2, wa, wb, b, offs, offs2, out_0, out_1, out_2
):
    nc = tc.nc
    with ExitStack() as ctx:
        lists = ctx.enter_context(tc.tile_pool(name="lists", bufs=1))
        keep = ctx.enter_context(tc.tile_pool(name="keep", bufs=1))
        psum = ctx.enter_context(tc.psum_pool(name="psum", bufs=8))

        def load_rows(src, i, name):
            rows = keep.tile([P, T], F32, name=name, tag=name, align_bytes=64)
            nc.sync.dma_start(out=rows[:], in_=src.rearrange("(p i) t -> p i t", i=PACK)[:, i, :])
            return rows

        def load_weight(src, name):
            raw = keep.tile([P, PACK, N], F32, name=name, tag=name, align_bytes=64)
            nc.sync.dma_start(out=raw[:], in_=src.rearrange("(p i) n -> p i n", i=PACK))
            return raw

        def gather(picked, i, rows, offsets, gain, j0, width):
            cols = slice(j0, j0 + width)
            nc.vector.tensor_tensor(
                picked[:, i, cols],
                rows[:].indirect(offsets[:, j0 // LIST_ROWS : (j0 + width) // LIST_ROWS]),
                gain[:, cols],
                MULT,
            )

        def copy_on(engine, out, in_):
            if engine == "scalar":
                nc.scalar.copy(out, in_)
            else:
                nc.vector.tensor_copy(out, in_)

        def weave(engine, src, name):
            width = src.shape[2]
            woven = keep.tile([P, width * PACK], BF16, name=name, align_bytes=64)
            copy_on(
                engine,
                woven[:].rearrange("p (c r i) -> p c i r", r=RUN, i=PACK),
                src.rearrange("p i (c r) -> p c i r", r=RUN),
            )
            return woven

        def weave_weight(engine, raw, name):
            woven = keep.tile([P, N * PACK], BF16, name=name, align_bytes=64)
            copy_on(
                engine,
                woven[:].rearrange("p (t m i) -> p m i t", t=PACK, i=PACK),
                raw[:].rearrange("p i (m t) -> p m i t", t=PACK),
            )
            return woven

        def quantize(woven, name, slot=None):
            width = woven.shape[1] // PACK
            codes = keep.tile([P, width], U32, name=name + "_codes", tag=slot or name + "_codes", align_bytes=64)
            scales = keep.tile([P, width], U8, name=name + "_scales", align_bytes=64)
            nc.vector.quantize_mx(out=codes[:].bitcast(FP8X4), scales=scales[:], in_=woven[:])
            return codes, scales

        def project(acc, weight, t, moving):
            cols = slice(t * P, (t + 1) * P)
            nc.tensor.matmul_mx(
                out=acc,
                lhsT=weight[0][:, cols].bitcast(FP8X4),
                lhsT_scale=weight[1][:, cols],
                rhs=moving[0][:].bitcast(FP8X4),
                rhs_scale=moving[1][:],
                start=True,
                stop=True,
            )

        x_list = lists.tile([P, J // LIST_ROWS], U16, name="x_list")
        z_list = lists.tile([P, J // LIST_ROWS], U16, name="z_list")
        bias = keep.tile([P, PACK], F32, name="bias")
        x_gain = keep.tile([P, J], F32, name="x_gain")
        z_gain = keep.tile([P, J], F32, name="z_gain")
        per_turn = BANK // P
        live = HEADS * SEGS
        folded = keep.tile([P, P], F32, name="folded")
        nc.gpsimd.memset(folded[live:P, :], 0.0)
        nc.sync.dma_start(x_list[:], offs)
        nc.sync.dma_start(out=x_gain[:, 0:BANK], in_=wgt[:, 0:BANK])
        x_rows = [load_rows(xT, 0, "x_rows0")]
        nc.sync.dma_start(out=x_gain[:, BANK:J], in_=wgt[:, BANK:J])
        nc.sync.dma_start(
            out=folded[0:live, :], in_=wgt2.rearrange("(g s) (r c) -> s g r c", s=LIST_ROWS, c=P)[0]
        )
        for i in range(1, PACK):
            x_rows.append(load_rows(xT, i, "x_rows%d" % i))
        nc.sync.dma_start(z_list[:], offs2)
        nc.sync.dma_start(out=bias[:], in_=b.rearrange("(p t) -> p t", t=PACK))
        wa_raw = load_weight(wa, "wa_raw")
        z_rows = [load_rows(zT, i, "z_rows%d" % i) for i in range(2)]
        wb_raw = load_weight(wb, "wb_raw")
        for i in range(2, PACK):
            z_rows.append(load_rows(zT, i, "z_rows%d" % i))

        ident = keep.tile([P, P], F32, name="ident")
        make_identity(nc, ident[:])
        warm = keep.tile([P, 1], F32, name="warm")
        nc.scalar.activation(warm[:], ident[:, 0:1], SILU)

        turned = psum.tile([P, BANK], F32, name="acc")
        nc.tensor.transpose(turned[:, 0:P], folded[:], ident[:])
        by_seg = turned[:, 0:live].rearrange("c (g r) -> c r g", r=SEGS)
        spread = keep.tile([P, SEGS, P], F32, name="spread")
        nc.scalar.copy(
            spread[:].rearrange("c r (g s) -> c r g s", s=LIST_ROWS),
            by_seg.unsqueeze(3).to_broadcast([P, SEGS, HEADS, LIST_ROWS]),
        )
        for h in range(SEGS // per_turn):
            back = psum.tile([P, BANK], F32, name="acc")
            for r in range(per_turn):
                nc.tensor.transpose(back[:, r * P : (r + 1) * P], spread[:, h * per_turn + r, :], ident[:])
            nc.scalar.copy(z_gain[:, h * BANK : (h + 1) * BANK], back[:])

        x_picked = keep.tile([P, PACK, J], F32, name="x_picked")
        gather(x_picked, 0, x_rows[0], x_list, x_gain, 0, J // 2)
        gather(x_picked, 0, x_rows[0], x_list, x_gain, J // 2, J // 2)
        gather(x_picked, 1, x_rows[1], x_list, x_gain, 0, J)
        gather(x_picked, 2, x_rows[2], x_list, x_gain, 0, J)
        x_woven = []
        for c in range(J // X_CHUNK):
            gather(x_picked, 3, x_rows[3], x_list, x_gain, c * X_CHUNK, X_CHUNK)
            x_woven.append(weave("scalar", x_picked[:, :, c * X_CHUNK : (c + 1) * X_CHUNK], "x_woven%d" % c))
        wa_mx = quantize(weave_weight("vector", wa_raw, "wa_woven"), "wa")
        z_picked = keep.tile([P, PACK, J], F32, name="z_picked")
        gather(z_picked, 0, z_rows[0], z_list, z_gain, 0, J)
        ya = keep.tile([P, PACK, J], F32, name="ya")
        for c in range(J // X_CHUNK):
            x_mx = quantize(x_woven[c], "x%d" % c, ("wa_raw", "z_rows0")[c])
            for t in range(PACK):
                acc = psum.tile([P, BANK], F32, name="acc")
                project(acc[:], wa_mx, t, x_mx)
                nc.scalar.copy(ya[:, t, c * X_CHUNK : (c + 1) * X_CHUNK], acc[:])

        for i in range(1, PACK - 1):
            gather(z_picked, i, z_rows[i], z_list, z_gain, 0, J)
        wb_woven = weave_weight("scalar", wb_raw, "wb_woven")
        spans = [slice(sum(Z_WIDTHS[:c]), sum(Z_WIDTHS[: c + 1])) for c in range(len(Z_WIDTHS))]
        z_woven = []
        for c, cols in enumerate(spans):
            gather(z_picked, 3, z_rows[3], z_list, z_gain, cols.start, Z_WIDTHS[c])
            z_woven.append(weave("scalar", z_picked[:, :, cols], "z_woven%d" % c))
        wb_mx = quantize(wb_woven, "wb", "z_rows3")

        y_codes = keep.tile([P, J], U32, name="y_codes", align_bytes=64)
        y_scales = keep.tile([P, J], U8, name="y_scales", align_bytes=64)
        out_rows = out_0.rearrange("(p t) j -> p t j", t=PACK)
        out_words = out_1.rearrange("a p j i -> p (a j i)").bitcast(I32)
        out_scales = out_2.rearrange("a q j -> q (a j)").bitcast(I32)
        z_mx = [quantize(z_woven[c], "z%d" % c) for c in range(len(spans))]
        ys = []
        for c, cols in enumerate(spans):
            width = Z_WIDTHS[c]
            per_bank = BANK // width
            prod = keep.tile([P, PACK, width], F32, name="prod%d" % c)
            y = keep.tile([P, PACK, width], F32, name="y%d" % c)
            for t0 in range(0, PACK, per_bank):
                acc = psum.tile([P, BANK], F32, name="acc")
                for u in range(per_bank):
                    project(acc[:, u * width : (u + 1) * width], wb_mx, t0 + u, z_mx[c])
                nc.vector.tensor_tensor(
                    prod[:, t0 : t0 + per_bank, :],
                    acc[:].rearrange("p (u j) -> p u j", u=per_bank),
                    ya[:, t0 : t0 + per_bank, cols],
                    MULT,
                )
                for t in range(t0, t0 + per_bank):
                    nc.scalar.activation(y[:, t, :], prod[:, t, :], SILU, bias=bias[:, t : t + 1])
            nc.sync.dma_start(out=out_rows[:, :, cols], in_=y[:])
            ys.append(y)
        for c, cols in enumerate(spans):
            y_woven = weave("scalar" if c == 0 else "vector", ys[c][:], "y_woven%d" % c)
            nc.vector.quantize_mx(out=y_codes[:, cols].bitcast(FP8X4), scales=y_scales[:, cols], in_=y_woven[:])
            nc.sync.dma_start(out=out_words[:, cols], in_=y_codes[:, cols].bitcast(I32))
        for q in range(4):
            queue = nc.sync if q % 2 == 0 else nc.scalar
            queue.dma_start(out=out_scales[4 * q : 4 * q + 4, :], in_=y_scales[32 * q : 32 * q + 4, :].bitcast(I32))
